import numpy as np
import ml_dtypes


def mxq(x, axis, fmt="e4m3"):
    dtype, down = {"e4m3": (ml_dtypes.float8_e4m3fn, 7), "e5m2": (ml_dtypes.float8_e5m2, 14)}[fmt]
    v = np.moveaxis(np.asarray(x, np.float32).astype(ml_dtypes.bfloat16).astype(np.float64), axis, -1)
    blocks = v.reshape(v.shape[:-1] + (-1, 32))
    amax = np.abs(blocks).max(-1, keepdims=True)
    byte = np.maximum(np.where(amax > 0, np.frexp(amax)[1] - 1 + 127, 0) - down, 1)
    scale = np.exp2(byte - 127.0)
    codes = (blocks / scale).astype(np.float32).astype(dtype).astype(np.float64)
    return np.moveaxis((codes * scale).reshape(v.shape), -1, axis)


WIDE = False


def mx_kscale(k):
    if not WIDE:
        return np.ones(k)
    levels = np.array([10, -10, 5, -5, 0])
    if k % 512:
        return np.exp2(np.random.permutation(np.resize(levels, k // 32))).repeat(32)
    a = np.empty((k // 512, 16))
    for p in range(k // 512):
        a[p, :8] = np.random.permutation(np.resize(levels, 8))
        for g in range(8):
            far = levels[np.abs(levels - a[p, g]) >= 10]
            a[p, g + 8] = far[np.random.randint(len(far))]
    return np.exp2(a.ravel()).repeat(32)


def f64(x):
    return np.asarray(x).astype(np.float64)


def striped(idx):
    return np.tile(idx.reshape(-1, 16).T, (8, 1)).astype(np.uint16)


def unstriped(offs):
    return offs[:16].T.reshape(-1).astype(np.int64)


def silu(v):
    return v / (1.0 + np.exp(-np.maximum(v, -700.0)))


K, T, S, H, N = 1024, 2048, 1024, 512, 256


def setup_inputs():
    n = np.random.standard_normal
    s = mx_kscale(K)[:, None]
    u = mx_kscale(H)
    return {
        "xT": (n((K, T)) * s).astype(np.float32),
        "w1": (n((K, H)) / np.sqrt(K) / s).astype(np.float32),
        "w3": (n((K, H)) / np.sqrt(K) / s * u).astype(np.float32),
        "w2": (n((H, N)) / np.sqrt(H) / u[:, None]).astype(np.float32),
        "offs": striped(np.random.permutation(T)[:S]),
    }


def reference(xT, w1, w3, w2, offs):
    idx = unstriped(offs)
    xq = mxq(f64(xT)[:, idx], 0, "e4m3")
    h = silu(mxq(f64(w1), 0, "e4m3").T @ xq) * (mxq(f64(w3), 0, "e4m3").T @ xq)
    y = mxq(f64(w2), 0, "e4m3").T @ mxq(h, 0, "e4m3")
    return y

@@ -1,0 +1,265 @@
+from contextlib import ExitStack
+
+import concourse.mybir as mybir
+from concourse.masks import make_identity
+
+K, T, S, H, N = 1024, 2048, 1024, 512, 256
+FLOPS = 2 * S * (2 * K * H + H * N)
+
+F32 = mybir.dt.float32
+BF16 = mybir.dt.bfloat16
+U32 = mybir.dt.uint32
+U16 = mybir.dt.uint16
+U8 = mybir.dt.uint8
+FP8X4 = mybir.dt.float8_e4m3fn_x4
+COPY = mybir.ActivationFunctionType.Copy
+SILU = mybir.ActivationFunctionType.Silu
+MULT = mybir.AluOpType.mult
+
+P = 128
+TC = 512
+XS = 256
+WS = {"w10": 320, "w11": 320, "w30": 192, "w31": 192}
+W2S = 128
+
+
+def tile_picked_pick_glu_silu_sub_e_kernel(tc, xT, w1, w3, w2, offs, out):
+    nc = tc.nc
+    with ExitStack() as ctx:
+        keep = ctx.enter_context(tc.tile_pool(name="keep", bufs=1))
+        grp = ctx.enter_context(tc.tile_pool(name="grp", bufs=4))
+        ring = ctx.enter_context(tc.tile_pool(name="ring", bufs=4))
+        pg = ctx.enter_context(tc.psum_pool(name="pg", bufs=3))
+        pu = ctx.enter_context(tc.psum_pool(name="pu", bufs=3))
+        py = ctx.enter_context(tc.psum_pool(name="py", bufs=2))
+
+        offsets = keep.tile([P, S // 16], U16, name="offsets")
+        nc.sync.dma_start(offsets[:], offs)
+
+        xbytes = keep.tile([P, T], U8, name="xbytes", align_bytes=256)
+        nc.gpsimd.memset(xbytes[:], 0)
+        warm = keep.tile([P, 16], F32, name="warm")
+        nc.gpsimd.memset(warm[:], 0.0)
+        nc.scalar.activation(warm[:], warm[:], SILU)
+
+        ident = keep.tile([P, P], F32, name="ident")
+        make_identity(nc, ident[:])
+
+        raw = {}
+
+        def load(key, src, width):
+            t = keep.tile([P, 4, width], F32, name="raw_" + key)
+            nc.sync.dma_start(t[:], src.rearrange("(p j) w -> p j w", j=4))
+            raw[key] = t
+
+        def load_x(s, c):
+            load("x%d%d" % (s, c), xT[512 * s : 512 * s + 512, TC * c : TC * c + TC], TC)
+
+        def load_w(name, w, s):
+            load(name + str(s), w[512 * s : 512 * s + 512, :], w.shape[1])
+
+        for s in range(2):
+            for c in range(T // TC):
+                load_x(s, c)
+        load_w("w1", w1, 0)
+        load_w("w1", w1, 1)
+        load_w("w3", w3, 0)
+        load_w("w3", w3, 1)
+        load_w("w2", w2, 0)
+
+        words = [keep.tile([P, T], U32, name="words%d" % s, align_bytes=256) for s in range(2)]
+        gwords = [keep.tile([P, S], U32, name="gwords%d" % s, align_bytes=256) for s in range(2)]
+        gbytes = keep.tile([P, S], U8, name="gbytes", align_bytes=256)
+
+        def round_x(s, c):
+            r = raw["x%d%d" % (s, c)]
+            g = grp.tile([P, TC, 4], BF16, name="gx", align_bytes=256)
+
+            def views(a, b):
+                dst = g[:, a:b, :].rearrange("p (c i) t -> p c t i", i=4)
+                return dst, r[:, :, a:b].rearrange("p t (c i) -> p c t i", i=4)
+
+            d, v = views(0, XS)
+            nc.scalar.activation(d, v, COPY)
+            d, v = views(XS, TC)
+            nc.vector.tensor_copy(d, v)
+            return g
+
+        def quant_x(s, c, g):
+            cols = slice(TC * c, TC * c + TC)
+            nc.vector.quantize_mx(
+                out=words[s][:, cols].bitcast(FP8X4),
+                scales=xbytes[4 * s : P, cols],
+                in_=g[:].rearrange("p w j -> p (w j)"),
+            )
+
+        def gather_words(s, a, b):
+            nc.vector.tensor_copy(gwords[s][:, a:b], words[s][:].indirect(offsets[:, a // 16 : b // 16]))
+
+        def gather_bytes(a, b):
+            nc.vector.tensor_copy(gbytes[:, a:b], xbytes[:].indirect(offsets[:, a // 16 : b // 16]))
+
+        def round_w(key):
+            r = raw[key]
+            g = grp.tile([P, 4, P, 4], BF16, name="gw", align_bytes=256)
+            src = r[:].rearrange("p j (m t) -> p m j t", t=4)
+            dst = g[:].rearrange("p t m j -> p m j t")
+            h = WS[key] // 4
+            nc.scalar.activation(dst[:, 0:h], src[:, 0:h], COPY)
+            nc.vector.tensor_copy(dst[:, h:P], src[:, h:P])
+            return g
+
+        wq = {}
+
+        def quant_w(key, g):
+            wc = keep.tile([P, H], U32, name="c_" + key, align_bytes=256)
+            wb = keep.tile([P, H], U8, name="b_" + key, align_bytes=256)
+            nc.vector.quantize_mx(
+                out=wc[:].bitcast(FP8X4), scales=wb[:], in_=g[:].rearrange("p t m j -> p (t m j)")
+            )
+            wq[key] = (wc, wb)
+
+        w2c = keep.tile([P, N], U32, name="w2c", align_bytes=256)
+        w2b = keep.tile([P, N], U8, name="w2b", align_bytes=256)
+
+        def round_w2():
+            r = raw["w20"]
+            g = grp.tile([P, N, 4], BF16, name="gw2", align_bytes=256, bufs=1)
+
+            def views(a, b):
+                dst = g[:, a:b, :].rearrange("p (c i) t -> p c t i", i=4)
+                return dst, r[:, :, a:b].rearrange("p t (c i) -> p c t i", i=4)
+
+            d, v = views(0, W2S)
+            nc.scalar.activation(d, v, COPY)
+            d, v = views(W2S, N)
+            nc.vector.tensor_copy(d, v)
+            return g
+
+        def quant_w2(g):
+            nc.vector.quantize_mx(
+                out=w2c[:].bitcast(FP8X4), scales=w2b[:], in_=g[:].rearrange("p w j -> p (w j)")
+            )
+
+        def warm_pe(key, count):
+            r = raw[key]
+            bank = pu.tile([P, 4, P], F32, name="up")
+            for i in range(count):
+                nc.tensor.transpose(bank[:, i % 4, :], r[:, i % 4, P * (i // 4 % 4) : P * (i // 4 % 4) + P], ident[:])
+
+        prev = None
+        for s in range(2):
+            for c in range(T // TC):
+                g = round_x(s, c)
+                if prev:
+                    quant_x(*prev)
+                prev = (s, c, g)
+                if s == 1 and c >= 1 and c <= 2:
+                    gather_words(0, 512 * (c - 1), 512 * c)
+        quant_x(*prev)
+
+        def gather_slice(i):
+            gather_words(1, 256 * i, 256 * i + 256)
+            gather_bytes(256 * i, 256 * i + 256)
+
+        gather_slice(0)
+        g0 = round_w("w10")
+        gather_slice(1)
+        g1 = round_w("w11")
+        warm_pe("w10", 16)
+        warm_pe("w11", 20)
+        quant_w("w10", g0)
+        quant_w("w11", g1)
+        gather_slice(2)
+        g0 = round_w("w30")
+        gather_slice(3)
+        quant_w("w30", g0)
+        g1 = round_w("w31")
+        quant_w("w31", g1)
+        g2 = round_w2()
+        quant_w2(g2)
+
+        def pass_mm(o, key, s, t, n0, n1, start, stop):
+            wc, wb = wq[key + str(s)]
+            nc.tensor.matmul_mx(
+                out=o,
+                lhsT=wc[:, P * t : P * t + P].bitcast(FP8X4),
+                lhsT_scale=wb[:, P * t : P * t + P],
+                rhs=gwords[s][:, n0:n1].bitcast(FP8X4),
+                rhs_scale=gbytes[4 * s : P, n0:n1],
+                start=start,
+                stop=stop,
+            )
+
+        sil = []
+        for n0 in range(0, S, 256):
+            sg = keep.tile([P, 4, 256], F32, name="sg%d" % n0)
+            for b in range(2):
+                bank = pg.tile([P, 2, 256], F32, name="gate")
+                for t in range(2):
+                    for s in range(2):
+                        pass_mm(bank[:, t, :], "w1", s, 2 * b + t, n0, n0 + 256, s == 0, s == 1)
+                nc.scalar.activation(sg[:, 2 * b : 2 * b + 2, :], bank[:], SILU)
+            sil.append(sg)
+
+        outv = out.rearrange("(m p) n -> p m n", p=P)
+        hq = {}
+
+        def up_mul(k):
+            n0 = P * k
+            bank = pu.tile([P, 4, P], F32, name="up")
+            for t in range(4):
+                for s in range(2):
+                    pass_mm(bank[:, t, :], "w3", s, t, n0, n0 + P, s == 0, s == 1)
+            h = ring.tile([P, P, 4], BF16, name="h", align_bytes=256)
+            o = n0 % 256
+            sg = sil[n0 // 256][:, :, o : o + P]
+            nc.vector.tensor_tensor(h[:], bank[:].rearrange("p t n -> p n t"), sg.rearrange("p t n -> p n t"), MULT)
+            return h
+
+        def quant_h(k, h, hc, hb, r):
+            cols = slice(P * r, P * r + P)
+            nc.vector.quantize_mx(
+                out=hc[:, cols].bitcast(FP8X4), scales=hb[:, cols], in_=h[:].rearrange("p n t -> p (n t)")
+            )
+
+        def layer2(n0, n, hc, hb):
+            y = py.tile([P, 2, n], F32, name="y")
+            for m in range(2):
+                nc.tensor.matmul_mx(
+                    out=y[:, m, :],
+                    lhsT=w2c[:, P * m : P * m + P].bitcast(FP8X4),
+                    lhsT_scale=w2b[:, P * m : P * m + P],
+                    rhs=hc[:, 0:n].bitcast(FP8X4),
+                    rhs_scale=hb[:, 0:n],
+                    start=True,
+                    stop=True,
+                )
+            yo = ring.tile([P, 2, n], F32, name="yo")
+            nc.scalar.activation(yo[:], y[:], COPY)
+            nc.sync.dma_start(outv[:, :, n0 : n0 + n], yo[:])
+
+        blocks = [2, 2, 2, 1, 1]
+        plan = []
+        k = 0
+        for n in blocks:
+            for r in range(n):
+                plan.append((k, n, r))
+                k += 1
+        pend = None
+
+        def finish(item):
+            kk, h, n, r, hc, hb = item
+            quant_h(kk, h, hc, hb, r)
+            if r == n - 1:
+                layer2(P * (kk - r), P * n, hc, hb)
+
+        for k, n, r in plan:
+            if r == 0:
+                hc = ring.tile([P, 256], U32, name="hc", align_bytes=256)
+                hb = ring.tile([P, 256], U8, name="hb", align_bytes=256)
+            h = up_mul(k)
+            if pend:
+                finish(pend)
+            pend = (k, h, n, r, hc, hb)
+        finish(pend)

@@ -1,7 +1,6 @@
 from contextlib import ExitStack
 
 import concourse.mybir as mybir
-from concourse.masks import make_identity
 
 K, T, S, H, N = 1024, 2048, 1024, 512, 256
 FLOPS = 2 * S * (2 * K * H + H * N)
@@ -18,16 +17,17 @@ MULT = mybir.AluOpType.mult
 
 P = 128
 TC = 512
-XS = 256
-WS = {"w10": 320, "w11": 320, "w30": 192, "w31": 192}
-W2S = 128
+XS = 288
+WS = {"w10": 320, "w11": 256, "w30": 256, "w31": 192}
+W2S = 256
 
 
 def tile_picked_pick_glu_silu_sub_e_kernel(tc, xT, w1, w3, w2, offs, out):
     nc = tc.nc
     with ExitStack() as ctx:
         keep = ctx.enter_context(tc.tile_pool(name="keep", bufs=1))
-        grp = ctx.enter_context(tc.tile_pool(name="grp", bufs=4))
+        grp = ctx.enter_context(tc.tile_pool(name="grp", bufs=2))
+        over = ctx.enter_context(tc.tile_pool(name="over", bufs=1))
         ring = ctx.enter_context(tc.tile_pool(name="ring", bufs=4))
         pg = ctx.enter_context(tc.psum_pool(name="pg", bufs=3))
         pu = ctx.enter_context(tc.psum_pool(name="pu", bufs=3))
@@ -42,25 +42,26 @@ def tile_picked_pick_glu_silu_sub_e_kernel(tc, xT, w1, w3, w2, offs, out):
         nc.gpsimd.memset(warm[:], 0.0)
         nc.scalar.activation(warm[:], warm[:], SILU)
 
-        ident = keep.tile([P, P], F32, name="ident")
-        make_identity(nc, ident[:])
-
         raw = {}
+        xpart = {}
+        loaded = []
 
         def load(key, src, width):
-            t = keep.tile([P, 4, width], F32, name="raw_" + key)
+            t = keep.tile([P, 4, width], F32, name="raw_%s_%d" % (key, len(loaded)))
+            loaded.append(key)
             nc.sync.dma_start(t[:], src.rearrange("(p j) w -> p j w", j=4))
             raw[key] = t
 
-        def load_x(s, c):
-            load("x%d%d" % (s, c), xT[512 * s : 512 * s + 512, TC * c : TC * c + TC], TC)
+        def load_x(s, c, n):
+            load("x%d" % s, xT[512 * s : 512 * s + 512, TC * c : TC * (c + n)], TC * n)
+            for i in range(n):
+                xpart[s, c + i] = raw["x%d" % s][:, :, TC * i : TC * i + TC]
 
         def load_w(name, w, s):
             load(name + str(s), w[512 * s : 512 * s + 512, :], w.shape[1])
 
-        for s in range(2):
-            for c in range(T // TC):
-                load_x(s, c)
+        for s, c, n in ((0, 0, 1), (0, 1, 1), (0, 2, 2), (1, 0, 2), (1, 2, 1), (1, 3, 1)):
+            load_x(s, c, n)
         load_w("w1", w1, 0)
         load_w("w1", w1, 1)
         load_w("w3", w3, 0)
@@ -68,12 +69,18 @@ def tile_picked_pick_glu_silu_sub_e_kernel(tc, xT, w1, w3, w2, offs, out):
         load_w("w2", w2, 0)
 
         words = [keep.tile([P, T], U32, name="words%d" % s, align_bytes=256) for s in range(2)]
-        gwords = [keep.tile([P, S], U32, name="gwords%d" % s, align_bytes=256) for s in range(2)]
-        gbytes = keep.tile([P, S], U8, name="gbytes", align_bytes=256)
+        gwords0 = keep.tile([P, S], U32, name="gwords0", align_bytes=256)
+        halves = []
+
+        x_last = over.tile([P, 2 * TC, 4], BF16, name="x_last", align_bytes=256, offset=0)
+        place = {"w10": 0, "w11": 4096, "w30": 0, "w31": 6656}
 
         def round_x(s, c):
-            r = raw["x%d%d" % (s, c)]
-            g = grp.tile([P, TC, 4], BF16, name="gx", align_bytes=256)
+            r = xpart[s, c]
+            if s == 1 and c >= 2:
+                g = x_last[:, TC * (c - 2) : TC * (c - 1), :]
+            else:
+                g = grp.tile([P, TC, 4], BF16, name="gx", align_bytes=256)
 
             def views(a, b):
                 dst = g[:, a:b, :].rearrange("p (c i) t -> p c t i", i=4)
@@ -90,18 +97,22 @@ def tile_picked_pick_glu_silu_sub_e_kernel(tc, xT, w1, w3, w2, offs, out):
             nc.vector.quantize_mx(
                 out=words[s][:, cols].bitcast(FP8X4),
                 scales=xbytes[4 * s : P, cols],
-                in_=g[:].rearrange("p w j -> p (w j)"),
+                in_=g[:, :, :].rearrange("p w j -> p (w j)"),
             )
 
-        def gather_words(s, a, b):
-            nc.vector.tensor_copy(gwords[s][:, a:b], words[s][:].indirect(offsets[:, a // 16 : b // 16]))
+        def gather(dst, window, a, b):
+            nc.vector.tensor_copy(dst, window[:].indirect(offsets[:, a // 16 : b // 16]))
 
-        def gather_bytes(a, b):
-            nc.vector.tensor_copy(gbytes[:, a:b], xbytes[:].indirect(offsets[:, a // 16 : b // 16]))
+        def moving(s, n0, n1):
+            h, a = n0 // 512, n0 % 512
+            words1, bytes01 = halves[h]
+            b = a + n1 - n0
+            codes = gwords0[:, n0:n1] if s == 0 else words1[:, a:b]
+            return codes.bitcast(FP8X4), bytes01[4 * s : P, a:b]
 
         def round_w(key):
             r = raw[key]
-            g = grp.tile([P, 4, P, 4], BF16, name="gw", align_bytes=256)
+            g = over.tile([P, 4, P, 4], BF16, name="g_" + key, align_bytes=256, offset=place[key])
             src = r[:].rearrange("p j (m t) -> p m j t", t=4)
             dst = g[:].rearrange("p t m j -> p m j t")
             h = WS[key] // 4
@@ -124,7 +135,7 @@ def tile_picked_pick_glu_silu_sub_e_kernel(tc, xT, w1, w3, w2, offs, out):
 
         def round_w2():
             r = raw["w20"]
-            g = grp.tile([P, N, 4], BF16, name="gw2", align_bytes=256, bufs=1)
+            g = over.tile([P, N, 4], BF16, name="gw2", align_bytes=256, offset=0)
 
             def views(a, b):
                 dst = g[:, a:b, :].rearrange("p (c i) t -> p c t i", i=4)
@@ -132,20 +143,12 @@ def tile_picked_pick_glu_silu_sub_e_kernel(tc, xT, w1, w3, w2, offs, out):
 
             d, v = views(0, W2S)
             nc.scalar.activation(d, v, COPY)
-            d, v = views(W2S, N)
-            nc.vector.tensor_copy(d, v)
             return g
 
         def quant_w2(g):
             nc.vector.quantize_mx(
                 out=w2c[:].bitcast(FP8X4), scales=w2b[:], in_=g[:].rearrange("p w j -> p (w j)")
             )
-
-        def warm_pe(key, count):
-            r = raw[key]
-            bank = pu.tile([P, 4, P], F32, name="up")
-            for i in range(count):
-                nc.tensor.transpose(bank[:, i % 4, :], r[:, i % 4, P * (i // 4 % 4) : P * (i // 4 % 4) + P], ident[:])
 
         prev = None
         for s in range(2):
@@ -155,19 +158,27 @@ def tile_picked_pick_glu_silu_sub_e_kernel(tc, xT, w1, w3, w2, offs, out):
                     quant_x(*prev)
                 prev = (s, c, g)
                 if s == 1 and c >= 1 and c <= 2:
-                    gather_words(0, 512 * (c - 1), 512 * c)
+                    gather(gwords0[:, 512 * (c - 1) : 512 * c], words[0], 512 * (c - 1), 512 * c)
         quant_x(*prev)
 
         def gather_slice(i):
-            gather_words(1, 256 * i, 256 * i + 256)
-            gather_bytes(256 * i, 256 * i + 256)
+            if i == 0:
+                words1 = keep.tile([P, 512], U32, name="words1_a", align_bytes=256)
+                bytes01 = keep.tile([P, 512], U8, name="bytes01_a", align_bytes=256)
+                halves.append((words1, bytes01))
+            if i == 2:
+                words1 = over.tile([P, 512], U32, name="words1_b", align_bytes=256, offset=4096)
+                bytes01 = over.tile([P, 512], U8, name="bytes01_b", align_bytes=256, offset=6144)
+                halves.append((words1, bytes01))
+            words1, bytes01 = halves[i // 2]
+            a = 256 * (i % 2)
+            gather(words1[:, a : a + 256], words[1], 256 * i, 256 * i + 256)
+            gather(bytes01[:, a : a + 256], xbytes, 256 * i, 256 * i + 256)
 
         gather_slice(0)
         g0 = round_w("w10")
         gather_slice(1)
         g1 = round_w("w11")
-        warm_pe("w10", 16)
-        warm_pe("w11", 20)
         quant_w("w10", g0)
         quant_w("w11", g1)
         gather_slice(2)
@@ -181,12 +192,13 @@ def tile_picked_pick_glu_silu_sub_e_kernel(tc, xT, w1, w3, w2, offs, out):
 
         def pass_mm(o, key, s, t, n0, n1, start, stop):
             wc, wb = wq[key + str(s)]
+            codes, scales = moving(s, n0, n1)
             nc.tensor.matmul_mx(
                 out=o,
                 lhsT=wc[:, P * t : P * t + P].bitcast(FP8X4),
                 lhsT_scale=wb[:, P * t : P * t + P],
-                rhs=gwords[s][:, n0:n1].bitcast(FP8X4),
-                rhs_scale=gbytes[4 * s : P, n0:n1],
+                rhs=codes,
+                rhs_scale=scales,
                 start=start,
                 stop=stop,
             )
@@ -214,7 +226,12 @@ def tile_picked_pick_glu_silu_sub_e_kernel(tc, xT, w1, w3, w2, offs, out):
             h = ring.tile([P, P, 4], BF16, name="h", align_bytes=256)
             o = n0 % 256
             sg = sil[n0 // 256][:, :, o : o + P]
-            nc.vector.tensor_tensor(h[:], bank[:].rearrange("p t n -> p n t"), sg.rearrange("p t n -> p n t"), MULT)
+            nc.vector.tensor_tensor(
+                h[:].rearrange("p (c i) t -> p c t i", i=4),
+                bank[:].rearrange("p t (c i) -> p c t i", i=4),
+                sg.rearrange("p t (c i) -> p c t i", i=4),
+                MULT,
+            )
             return h
 
         def quant_h(k, h, hc, hb, r):

@@ -14,12 +14,12 @@ FP8X4 = mybir.dt.float8_e4m3fn_x4
 COPY = mybir.ActivationFunctionType.Copy
 SILU = mybir.ActivationFunctionType.Silu
 MULT = mybir.AluOpType.mult
+ADD = mybir.AluOpType.add
 
 P = 128
 TC = 512
 XS = 288
-WS = {"w10": 320, "w11": 256, "w30": 256, "w31": 192}
-W2S = 256
+WS = {"w10": (384, 0), "w11": (256, 64), "w30": (0, 256), "w31": (0, 192)}
 
 
 def tile_picked_pick_glu_silu_sub_e_kernel(tc, xT, w1, w3, w2, offs, out):
@@ -34,7 +34,6 @@ def tile_picked_pick_glu_silu_sub_e_kernel(tc, xT, w1, w3, w2, offs, out):
         py = ctx.enter_context(tc.psum_pool(name="py", bufs=2))
 
         offsets = keep.tile([P, S // 16], U16, name="offsets")
-        nc.sync.dma_start(offsets[:], offs)
 
         xbytes = keep.tile([P, T], U8, name="xbytes", align_bytes=256)
         nc.gpsimd.memset(xbytes[:], 0)
@@ -60,8 +59,10 @@ def tile_picked_pick_glu_silu_sub_e_kernel(tc, xT, w1, w3, w2, offs, out):
         def load_w(name, w, s):
             load(name + str(s), w[512 * s : 512 * s + 512, :], w.shape[1])
 
-        for s, c, n in ((0, 0, 1), (0, 1, 1), (0, 2, 2), (1, 0, 2), (1, 2, 1), (1, 3, 1)):
+        for s, c, n in ((0, 0, 2), (0, 2, 2), (1, 0, 2), (1, 2, 1), (1, 3, 1)):
             load_x(s, c, n)
+            if (s, c) == (0, 0):
+                nc.sync.dma_start(offsets[:], offs)
         load_w("w1", w1, 0)
         load_w("w1", w1, 1)
         load_w("w3", w3, 0)
@@ -115,9 +116,18 @@ def tile_picked_pick_glu_silu_sub_e_kernel(tc, xT, w1, w3, w2, offs, out):
             g = over.tile([P, 4, P, 4], BF16, name="g_" + key, align_bytes=256, offset=place[key])
             src = r[:].rearrange("p j (m t) -> p m j t", t=4)
             dst = g[:].rearrange("p t m j -> p m j t")
-            h = WS[key] // 4
-            nc.scalar.activation(dst[:, 0:h], src[:, 0:h], COPY)
-            nc.vector.tensor_copy(dst[:, h:P], src[:, h:P])
+            a = WS[key][0] // 4
+            b = a + WS[key][1] // 4
+            if a > 0:
+                nc.scalar.activation(dst[:, 0:a], src[:, 0:a], COPY)
+            if b > a:
+                nc.gpsimd.tensor_scalar(
+                    g[:, :, a:b, :],
+                    r[:].rearrange("p j (m t) -> p t m j", t=4)[:, :, a:b, :],
+                    1.0, 0.0, MULT, ADD,
+                )
+            if P > b:
+                nc.vector.tensor_copy(dst[:, b:P], src[:, b:P])
             return g
 
         wq = {}
@@ -136,13 +146,7 @@ def tile_picked_pick_glu_silu_sub_e_kernel(tc, xT, w1, w3, w2, offs, out):
         def round_w2():
             r = raw["w20"]
             g = over.tile([P, N, 4], BF16, name="gw2", align_bytes=256, offset=0)
-
-            def views(a, b):
-                dst = g[:, a:b, :].rearrange("p (c i) t -> p c t i", i=4)
-                return dst, r[:, :, a:b].rearrange("p t (c i) -> p c t i", i=4)
-
-            d, v = views(0, W2S)
-            nc.scalar.activation(d, v, COPY)
+            nc.gpsimd.tensor_scalar(g[:], r[:].rearrange("p t w -> p w t"), 1.0, 0.0, MULT, ADD)
             return g
 
         def quant_w2(g):
@@ -161,34 +165,27 @@ def tile_picked_pick_glu_silu_sub_e_kernel(tc, xT, w1, w3, w2, offs, out):
                     gather(gwords0[:, 512 * (c - 1) : 512 * c], words[0], 512 * (c - 1), 512 * c)
         quant_x(*prev)
 
-        def gather_slice(i):
+        def gather_half(i):
             if i == 0:
                 words1 = keep.tile([P, 512], U32, name="words1_a", align_bytes=256)
                 bytes01 = keep.tile([P, 512], U8, name="bytes01_a", align_bytes=256)
-                halves.append((words1, bytes01))
-            if i == 2:
+            else:
                 words1 = over.tile([P, 512], U32, name="words1_b", align_bytes=256, offset=4096)
                 bytes01 = over.tile([P, 512], U8, name="bytes01_b", align_bytes=256, offset=6144)
-                halves.append((words1, bytes01))
-            words1, bytes01 = halves[i // 2]
-            a = 256 * (i % 2)
-            gather(words1[:, a : a + 256], words[1], 256 * i, 256 * i + 256)
-            gather(bytes01[:, a : a + 256], xbytes, 256 * i, 256 * i + 256)
+            halves.append((words1, bytes01))
+            gather(words1[:], words[1], 512 * i, 512 * i + 512)
+            gather(bytes01[:], xbytes, 512 * i, 512 * i + 512)
 
-        gather_slice(0)
+        gather_half(0)
         g0 = round_w("w10")
-        gather_slice(1)
         g1 = round_w("w11")
         quant_w("w10", g0)
         quant_w("w11", g1)
-        gather_slice(2)
         g0 = round_w("w30")
-        gather_slice(3)
-        quant_w("w30", g0)
+        gather_half(1)
         g1 = round_w("w31")
+        quant_w("w30", g0)
         quant_w("w31", g1)
-        g2 = round_w2()
-        quant_w2(g2)
 
         def pass_mm(o, key, s, t, n0, n1, start, stop):
             wc, wb = wq[key + str(s)]
@@ -214,37 +211,37 @@ def tile_picked_pick_glu_silu_sub_e_kernel(tc, xT, w1, w3, w2, offs, out):
                 nc.scalar.activation(sg[:, 2 * b : 2 * b + 2, :], bank[:], SILU)
             sil.append(sg)
 
+        g2 = round_w2()
+        quant_w2(g2)
+
         outv = out.rearrange("(m p) n -> p m n", p=P)
         hq = {}
 
-        def up_mul(k):
+        def up_mul(k, h):
             n0 = P * k
             bank = pu.tile([P, 4, P], F32, name="up")
             for t in range(4):
                 for s in range(2):
                     pass_mm(bank[:, t, :], "w3", s, t, n0, n0 + P, s == 0, s == 1)
-            h = ring.tile([P, P, 4], BF16, name="h", align_bytes=256)
             o = n0 % 256
             sg = sil[n0 // 256][:, :, o : o + P]
             nc.vector.tensor_tensor(
-                h[:].rearrange("p (c i) t -> p c t i", i=4),
+                h.rearrange("p (c i) t -> p c t i", i=4),
                 bank[:].rearrange("p t (c i) -> p c t i", i=4),
                 sg.rearrange("p t (c i) -> p c t i", i=4),
                 MULT,
             )
-            return h
-
-        def quant_h(k, h, hc, hb, r):
-            cols = slice(P * r, P * r + P)
-            nc.vector.quantize_mx(
-                out=hc[:, cols].bitcast(FP8X4), scales=hb[:, cols], in_=h[:].rearrange("p n t -> p (n t)")
-            )
 
         def layer2(n0, n, hc, hb):
+            last = n0 + n == S
             y = py.tile([P, 2, n], F32, name="y")
+            outs = [y[:, 0, :], y[:, 1, :]]
+            if last:
+                y2 = py.tile([P, n], F32, name="y2", tag="y")
+                outs[1] = y2[:]
             for m in range(2):
                 nc.tensor.matmul_mx(
-                    out=y[:, m, :],
+                    out=outs[m],
                     lhsT=w2c[:, P * m : P * m + P].bitcast(FP8X4),
                     lhsT_scale=w2b[:, P * m : P * m + P],
                     rhs=hc[:, 0:n].bitcast(FP8X4),
@@ -252,31 +249,40 @@ def tile_picked_pick_glu_silu_sub_e_kernel(tc, xT, w1, w3, w2, offs, out):
                     start=True,
                     stop=True,
                 )
-            yo = ring.tile([P, 2, n], F32, name="yo")
-            nc.scalar.activation(yo[:], y[:], COPY)
-            nc.sync.dma_start(outv[:, :, n0 : n0 + n], yo[:])
+            if last:
+                yo0 = ring.tile([P, n], F32, name="yo0")
+                yo1 = ring.tile([P, n], F32, name="yo1")
+                nc.scalar.activation(yo0[:], outs[0], COPY)
+                nc.sync.dma_start(outv[:, 0, n0 : n0 + n], yo0[:])
+                nc.vector.tensor_copy(yo1[:], outs[1])
+                nc.sync.dma_start(outv[:, 1, n0 : n0 + n], yo1[:])
+            else:
+                yo = ring.tile([P, 2, n], F32, name="yo")
+                nc.scalar.activation(yo[:], y[:], COPY)
+                nc.sync.dma_start(outv[:, :, n0 : n0 + n], yo[:])
 
         blocks = [2, 2, 2, 1, 1]
-        plan = []
-        k = 0
-        for n in blocks:
-            for r in range(n):
-                plan.append((k, n, r))
-                k += 1
         pend = None
 
         def finish(item):
-            kk, h, n, r, hc, hb = item
-            quant_h(kk, h, hc, hb, r)
-            if r == n - 1:
-                layer2(P * (kk - r), P * n, hc, hb)
+            k, n, h = item
+            hc = ring.tile([P, 256], U32, name="hc", align_bytes=256)
+            hb = ring.tile([P, 256], U8, name="hb", align_bytes=256)
+            nc.vector.quantize_mx(
+                out=hc[:, 0 : P * n].bitcast(FP8X4),
+                scales=hb[:, 0 : P * n],
+                in_=h[:, 0 : P * n, :].rearrange("p n t -> p (n t)"),
+            )
+            layer2(P * k, P * n, hc, hb)
 
-        for k, n, r in plan:
-            if r == 0:
-                hc = ring.tile([P, 256], U32, name="hc", align_bytes=256)
-                hb = ring.tile([P, 256], U8, name="hb", align_bytes=256)
-            h = up_mul(k)
-            if pend:
-                finish(pend)
-            pend = (k, h, n, r, hc, hb)
+        k = 0
+        for n in blocks:
+            h = ring.tile([P, 256, 4], BF16, name="h", align_bytes=256)
+            for r in range(n):
+                up_mul(k + r, h[:, P * r : P * r + P, :])
+                if pend:
+                    finish(pend)
+                    pend = None
+            pend = (k, n, h)
+            k += n
         finish(pend)

@@ -14,275 +14,232 @@ FP8X4 = mybir.dt.float8_e4m3fn_x4
 COPY = mybir.ActivationFunctionType.Copy
 SILU = mybir.ActivationFunctionType.Silu
 MULT = mybir.AluOpType.mult
-ADD = mybir.AluOpType.add
 
 P = 128
-TC = 512
-XS = 288
-WS = {"w10": (384, 0), "w11": (256, 64), "w30": (0, 256), "w31": (0, 192)}
+PACK = 4
+KP = P * PACK
+CHUNK = 512
+HALF = 512
+BLOCK = 256
+
+TOKEN_LOADS = ((1024, 1024), (1024, 512, 512))
+X_SCALAR = 288
+W_SCALAR = {"w1_0": 384, "w1_1": 320, "w3_0": 384, "w3_1": 0}
+W2_SCALAR = 128
 
 
 def tile_picked_pick_glu_silu_sub_e_kernel(tc, xT, w1, w3, w2, offs, out):
     nc = tc.nc
     with ExitStack() as ctx:
         keep = ctx.enter_context(tc.tile_pool(name="keep", bufs=1))
-        grp = ctx.enter_context(tc.tile_pool(name="grp", bufs=2))
-        over = ctx.enter_context(tc.tile_pool(name="over", bufs=1))
-        ring = ctx.enter_context(tc.tile_pool(name="ring", bufs=4))
-        pg = ctx.enter_context(tc.psum_pool(name="pg", bufs=3))
-        pu = ctx.enter_context(tc.psum_pool(name="pu", bufs=3))
-        py = ctx.enter_context(tc.psum_pool(name="py", bufs=2))
+        chunks = ctx.enter_context(tc.tile_pool(name="chunks", bufs=2))
+        turns = ctx.enter_context(tc.tile_pool(name="turns", bufs=1))
+        ring = ctx.enter_context(tc.tile_pool(name="ring", bufs=3))
+        gate_banks = ctx.enter_context(tc.psum_pool(name="gate_banks", bufs=3))
+        up_banks = ctx.enter_context(tc.psum_pool(name="up_banks", bufs=3))
+        out_banks = ctx.enter_context(tc.psum_pool(name="out_banks", bufs=2))
 
         offsets = keep.tile([P, S // 16], U16, name="offsets")
 
-        xbytes = keep.tile([P, T], U8, name="xbytes", align_bytes=256)
-        nc.gpsimd.memset(xbytes[:], 0)
-        warm = keep.tile([P, 16], F32, name="warm")
-        nc.gpsimd.memset(warm[:], 0.0)
-        nc.scalar.activation(warm[:], warm[:], SILU)
+        token_bytes = keep.tile([P, T], U8, name="token_bytes", align_bytes=256)
+        nc.gpsimd.memset(token_bytes[:], 0)
 
-        raw = {}
-        xpart = {}
-        loaded = []
+        first = keep.tile([P, 16], F32, name="first")
+        nc.gpsimd.memset(first[:], 0.0)
+        nc.scalar.activation(first[:], first[:], SILU)
 
-        def load(key, src, width):
-            t = keep.tile([P, 4, width], F32, name="raw_%s_%d" % (key, len(loaded)))
-            loaded.append(key)
-            nc.sync.dma_start(t[:], src.rearrange("(p j) w -> p j w", j=4))
-            raw[key] = t
+        def load(source, name):
+            tile = keep.tile([P, PACK, source.shape[1]], F32, name=name)
+            nc.sync.dma_start(tile[:], source.rearrange("(p j) c -> p j c", j=PACK))
+            return tile
 
-        def load_x(s, c, n):
-            load("x%d" % s, xT[512 * s : 512 * s + 512, TC * c : TC * (c + n)], TC * n)
-            for i in range(n):
-                xpart[s, c + i] = raw["x%d" % s][:, :, TC * i : TC * i + TC]
+        token_rows = {}
+        for s in range(2):
+            start = 0
+            for width in TOKEN_LOADS[s]:
+                tile = load(xT[KP * s : KP * s + KP, start : start + width], "x_%d_%d" % (s, start))
+                for a in range(0, width, CHUNK):
+                    token_rows[s, (start + a) // CHUNK] = tile[:, :, a : a + CHUNK]
+                if (s, start) == (0, 0):
+                    nc.sync.dma_start(offsets[:], offs)
+                start += width
+        weight_rows = {}
+        for name, w in (("w1", w1), ("w3", w3)):
+            for s in range(2):
+                key = "%s_%d" % (name, s)
+                weight_rows[key] = load(w[KP * s : KP * s + KP, :], key)
+        w2_rows = load(w2, "w2")
 
-        def load_w(name, w, s):
-            load(name + str(s), w[512 * s : 512 * s + 512, :], w.shape[1])
+        def round_columns(grouped, rows, split):
+            width = rows.shape[2]
+            for a, b in ((0, split), (split, width)):
+                if a < b:
+                    dst = grouped[:, a:b, :].rearrange("p (c i) j -> p c j i", i=4)
+                    src = rows[:, :, a:b].rearrange("p j (c i) -> p c j i", i=4)
+                    if a == 0:
+                        nc.scalar.activation(dst, src, COPY)
+                    else:
+                        nc.vector.tensor_copy(dst, src)
 
-        for s, c, n in ((0, 0, 2), (0, 2, 2), (1, 0, 2), (1, 2, 1), (1, 3, 1)):
-            load_x(s, c, n)
-            if (s, c) == (0, 0):
-                nc.sync.dma_start(offsets[:], offs)
-        load_w("w1", w1, 0)
-        load_w("w1", w1, 1)
-        load_w("w3", w3, 0)
-        load_w("w3", w3, 1)
-        load_w("w2", w2, 0)
-
-        words = [keep.tile([P, T], U32, name="words%d" % s, align_bytes=256) for s in range(2)]
-        gwords0 = keep.tile([P, S], U32, name="gwords0", align_bytes=256)
-        halves = []
-
-        x_last = over.tile([P, 2 * TC, 4], BF16, name="x_last", align_bytes=256, offset=0)
-        place = {"w10": 0, "w11": 4096, "w30": 0, "w31": 6656}
-
-        def round_x(s, c):
-            r = xpart[s, c]
-            if s == 1 and c >= 2:
-                g = x_last[:, TC * (c - 2) : TC * (c - 1), :]
-            else:
-                g = grp.tile([P, TC, 4], BF16, name="gx", align_bytes=256)
-
-            def views(a, b):
-                dst = g[:, a:b, :].rearrange("p (c i) t -> p c t i", i=4)
-                return dst, r[:, :, a:b].rearrange("p t (c i) -> p c t i", i=4)
-
-            d, v = views(0, XS)
-            nc.scalar.activation(d, v, COPY)
-            d, v = views(XS, TC)
-            nc.vector.tensor_copy(d, v)
-            return g
-
-        def quant_x(s, c, g):
-            cols = slice(TC * c, TC * c + TC)
-            nc.vector.quantize_mx(
-                out=words[s][:, cols].bitcast(FP8X4),
-                scales=xbytes[4 * s : P, cols],
-                in_=g[:, :, :].rearrange("p w j -> p (w j)"),
-            )
-
-        def gather(dst, window, a, b):
-            nc.vector.tensor_copy(dst, window[:].indirect(offsets[:, a // 16 : b // 16]))
-
-        def moving(s, n0, n1):
-            h, a = n0 // 512, n0 % 512
-            words1, bytes01 = halves[h]
-            b = a + n1 - n0
-            codes = gwords0[:, n0:n1] if s == 0 else words1[:, a:b]
-            return codes.bitcast(FP8X4), bytes01[4 * s : P, a:b]
-
-        def round_w(key):
-            r = raw[key]
-            g = over.tile([P, 4, P, 4], BF16, name="g_" + key, align_bytes=256, offset=place[key])
-            src = r[:].rearrange("p j (m t) -> p m j t", t=4)
-            dst = g[:].rearrange("p t m j -> p m j t")
-            a = WS[key][0] // 4
-            b = a + WS[key][1] // 4
+        def round_channels(grouped, rows, split):
+            dst = grouped[:].rearrange("p t m j -> p m j t")
+            src = rows[:].rearrange("p j (m t) -> p m j t", t=PACK)
+            a = split // PACK
             if a > 0:
                 nc.scalar.activation(dst[:, 0:a], src[:, 0:a], COPY)
-            if b > a:
-                nc.gpsimd.tensor_scalar(
-                    g[:, :, a:b, :],
-                    r[:].rearrange("p j (m t) -> p t m j", t=4)[:, :, a:b, :],
-                    1.0, 0.0, MULT, ADD,
-                )
-            if P > b:
-                nc.vector.tensor_copy(dst[:, b:P], src[:, b:P])
-            return g
+            if a < P:
+                nc.vector.tensor_copy(dst[:, a:P], src[:, a:P])
 
-        wq = {}
+        def quantise(words, scale_bytes, grouped):
+            nc.vector.quantize_mx(out=words.bitcast(FP8X4), scales=scale_bytes, in_=grouped)
 
-        def quant_w(key, g):
-            wc = keep.tile([P, H], U32, name="c_" + key, align_bytes=256)
-            wb = keep.tile([P, H], U8, name="b_" + key, align_bytes=256)
-            nc.vector.quantize_mx(
-                out=wc[:].bitcast(FP8X4), scales=wb[:], in_=g[:].rearrange("p t m j -> p (t m j)")
-            )
-            wq[key] = (wc, wb)
+        token_words = [keep.tile([P, T], U32, name="token_words_%d" % s, align_bytes=256) for s in range(2)]
 
-        w2c = keep.tile([P, N], U32, name="w2c", align_bytes=256)
-        w2b = keep.tile([P, N], U8, name="w2b", align_bytes=256)
-
-        def round_w2():
-            r = raw["w20"]
-            g = over.tile([P, N, 4], BF16, name="gw2", align_bytes=256, offset=0)
-            nc.gpsimd.tensor_scalar(g[:], r[:].rearrange("p t w -> p w t"), 1.0, 0.0, MULT, ADD)
-            return g
-
-        def quant_w2(g):
-            nc.vector.quantize_mx(
-                out=w2c[:].bitcast(FP8X4), scales=w2b[:], in_=g[:].rearrange("p w j -> p (w j)")
+        def quantise_tokens(s, c, grouped):
+            cols = slice(CHUNK * c, CHUNK * c + CHUNK)
+            quantise(
+                token_words[s][:, cols], token_bytes[PACK * s : P, cols], grouped.rearrange("p c j -> p (c j)")
             )
 
-        prev = None
+        weight_codes = {}
+
+        def quantise_weight(key, grouped):
+            words = keep.tile([P, H], U32, name="words_" + key, align_bytes=256)
+            scale_bytes = keep.tile([P, H], U8, name="bytes_" + key, align_bytes=256)
+            quantise(words[:], scale_bytes[:], grouped[:].rearrange("p t m j -> p (t m j)"))
+            weight_codes[key] = (words, scale_bytes)
+
+        def gather(dst, window, first_entry):
+            entries = offsets[:, first_entry // 16 : (first_entry + HALF) // 16]
+            nc.vector.tensor_copy(dst, window[:].indirect(entries))
+
+        last_chunks = turns.tile([P, 2 * CHUNK, PACK], BF16, name="last_chunks", align_bytes=256, offset=0)
+
+        picked_words0 = keep.tile([P, S], U32, name="picked_words0", align_bytes=256)
+        waiting = None
         for s in range(2):
-            for c in range(T // TC):
-                g = round_x(s, c)
-                if prev:
-                    quant_x(*prev)
-                prev = (s, c, g)
-                if s == 1 and c >= 1 and c <= 2:
-                    gather(gwords0[:, 512 * (c - 1) : 512 * c], words[0], 512 * (c - 1), 512 * c)
-        quant_x(*prev)
+            for c in range(T // CHUNK):
+                if s == 1 and c >= 2:
+                    grouped = last_chunks[:, CHUNK * (c - 2) : CHUNK * (c - 1), :]
+                else:
+                    chunk = chunks.tile([P, CHUNK, PACK], BF16, name="chunk", align_bytes=256)
+                    grouped = chunk[:, :, :]
+                round_columns(grouped, token_rows[s, c], X_SCALAR)
+                if waiting:
+                    quantise_tokens(*waiting)
+                waiting = (s, c, grouped)
+                if s == 1 and c in (1, 2):
+                    gather(picked_words0[:, HALF * (c - 1) : HALF * c], token_words[0], HALF * (c - 1))
+        quantise_tokens(*waiting)
 
-        def gather_half(i):
-            if i == 0:
-                words1 = keep.tile([P, 512], U32, name="words1_a", align_bytes=256)
-                bytes01 = keep.tile([P, 512], U8, name="bytes01_a", align_bytes=256)
-            else:
-                words1 = over.tile([P, 512], U32, name="words1_b", align_bytes=256, offset=4096)
-                bytes01 = over.tile([P, 512], U8, name="bytes01_b", align_bytes=256, offset=6144)
-            halves.append((words1, bytes01))
-            gather(words1[:], words[1], 512 * i, 512 * i + 512)
-            gather(bytes01[:], xbytes, 512 * i, 512 * i + 512)
+        def grouped_weight(key, offset):
+            grouped = turns.tile([P, PACK, P, PACK], BF16, name="grouped_" + key, align_bytes=256, offset=offset)
+            round_channels(grouped, weight_rows[key], W_SCALAR[key])
+            return grouped
 
-        gather_half(0)
-        g0 = round_w("w10")
-        g1 = round_w("w11")
-        quant_w("w10", g0)
-        quant_w("w11", g1)
-        g0 = round_w("w30")
-        gather_half(1)
-        g1 = round_w("w31")
-        quant_w("w30", g0)
-        quant_w("w31", g1)
+        words1_a = keep.tile([P, HALF], U32, name="words1_a", align_bytes=256)
+        bytes_a = keep.tile([P, HALF], U8, name="bytes_a", align_bytes=256)
+        gather(words1_a[:], token_words[1], 0)
+        gather(bytes_a[:], token_bytes, 0)
+        grouped_w1_0 = grouped_weight("w1_0", 0)
+        grouped_w1_1 = grouped_weight("w1_1", 4096)
+        quantise_weight("w1_0", grouped_w1_0)
+        quantise_weight("w1_1", grouped_w1_1)
+        grouped_w3_0 = grouped_weight("w3_0", 0)
+        words1_b = turns.tile([P, HALF], U32, name="words1_b", align_bytes=256, offset=4096)
+        bytes_b = turns.tile([P, HALF], U8, name="bytes_b", align_bytes=256, offset=6144)
+        gather(words1_b[:], token_words[1], HALF)
+        gather(bytes_b[:], token_bytes, HALF)
+        grouped_w3_1 = grouped_weight("w3_1", 6656)
+        quantise_weight("w3_0", grouped_w3_0)
+        quantise_weight("w3_1", grouped_w3_1)
+        picked = ((words1_a, bytes_a), (words1_b, bytes_b))
 
-        def pass_mm(o, key, s, t, n0, n1, start, stop):
-            wc, wb = wq[key + str(s)]
-            codes, scales = moving(s, n0, n1)
-            nc.tensor.matmul_mx(
-                out=o,
-                lhsT=wc[:, P * t : P * t + P].bitcast(FP8X4),
-                lhsT_scale=wb[:, P * t : P * t + P],
-                rhs=codes,
-                rhs_scale=scales,
-                start=start,
-                stop=stop,
-            )
+        def first_layer(bank, name, t, n0, n):
+            half, a = divmod(n0, HALF)
+            words1, scale_bytes = picked[half]
+            moving = (picked_words0[:, n0 : n0 + n], words1[:, a : a + n])
+            cols = slice(P * t, P * t + P)
+            for s in range(2):
+                words, weight_bytes = weight_codes["%s_%d" % (name, s)]
+                nc.tensor.matmul_mx(
+                    out=bank,
+                    lhsT=words[:, cols].bitcast(FP8X4),
+                    lhsT_scale=weight_bytes[:, cols],
+                    rhs=moving[s].bitcast(FP8X4),
+                    rhs_scale=scale_bytes[PACK * s : P, a : a + n],
+                    start=s == 0,
+                    stop=s == 1,
+                )
 
-        sil = []
-        for n0 in range(0, S, 256):
-            sg = keep.tile([P, 4, 256], F32, name="sg%d" % n0)
-            for b in range(2):
-                bank = pg.tile([P, 2, 256], F32, name="gate")
-                for t in range(2):
-                    for s in range(2):
-                        pass_mm(bank[:, t, :], "w1", s, 2 * b + t, n0, n0 + 256, s == 0, s == 1)
-                nc.scalar.activation(sg[:, 2 * b : 2 * b + 2, :], bank[:], SILU)
-            sil.append(sg)
+        gates = []
+        for half in range(2):
+            gate = keep.tile([P, PACK, HALF], F32, name="gate_%d" % half)
+            for t in range(PACK):
+                gate_bank = gate_banks.tile([P, HALF], F32, name="gate_bank")
+                first_layer(gate_bank[:], "w1", t, HALF * half, HALF)
+                nc.scalar.activation(gate[:, t, :], gate_bank[:], SILU)
+            gates.append(gate)
 
-        g2 = round_w2()
-        quant_w2(g2)
+        grouped_w2 = turns.tile([P, N, PACK], BF16, name="grouped_w2", align_bytes=256, offset=0)
+        round_columns(grouped_w2[:, :, :], w2_rows[:, :, :], W2_SCALAR)
+        w2_words = keep.tile([P, N], U32, name="w2_words", align_bytes=256)
+        w2_bytes = keep.tile([P, N], U8, name="w2_bytes", align_bytes=256)
+        quantise(w2_words[:], w2_bytes[:], grouped_w2[:].rearrange("p c j -> p (c j)"))
 
-        outv = out.rearrange("(m p) n -> p m n", p=P)
-        hq = {}
+        out_rows = out.rearrange("(m p) n -> p m n", p=P)
 
-        def up_mul(k, h):
-            n0 = P * k
-            bank = pu.tile([P, 4, P], F32, name="up")
-            for t in range(4):
-                for s in range(2):
-                    pass_mm(bank[:, t, :], "w3", s, t, n0, n0 + P, s == 0, s == 1)
-            o = n0 % 256
-            sg = sil[n0 // 256][:, :, o : o + P]
+        def hidden_tokens(hidden, n0):
+            up_bank = up_banks.tile([P, PACK, P], F32, name="up_bank")
+            for t in range(PACK):
+                first_layer(up_bank[:, t, :], "w3", t, n0, P)
+            half, a = divmod(n0, HALF)
             nc.vector.tensor_tensor(
-                h.rearrange("p (c i) t -> p c t i", i=4),
-                bank[:].rearrange("p t (c i) -> p c t i", i=4),
-                sg.rearrange("p t (c i) -> p c t i", i=4),
+                hidden.rearrange("p (c i) t -> p c t i", i=4),
+                up_bank[:].rearrange("p t (c i) -> p c t i", i=4),
+                gates[half][:, :, a : a + P].rearrange("p t (c i) -> p c t i", i=4),
                 MULT,
             )
 
-        def layer2(n0, n, hc, hb):
-            last = n0 + n == S
-            y = py.tile([P, 2, n], F32, name="y")
-            outs = [y[:, 0, :], y[:, 1, :]]
+        def second_layer(n0, hidden):
+            words = ring.tile([P, BLOCK], U32, name="hidden_words", align_bytes=256)
+            scale_bytes = ring.tile([P, BLOCK], U8, name="hidden_bytes", align_bytes=256)
+            quantise(words[:], scale_bytes[:], hidden[:].rearrange("p n t -> p (n t)"))
+            result = ring.tile([P, N // P, BLOCK], F32, name="result")
+            last = n0 + BLOCK == S
             if last:
-                y2 = py.tile([P, n], F32, name="y2", tag="y")
-                outs[1] = y2[:]
+                banks = [out_banks.tile([P, BLOCK], F32, name="out_half_%d" % m, tag="out_bank") for m in range(2)]
+                targets = [bank[:] for bank in banks]
+            else:
+                bank = out_banks.tile([P, N // P, BLOCK], F32, name="out_bank", tag="out_bank")
+                targets = [bank[:, m, :] for m in range(2)]
             for m in range(2):
                 nc.tensor.matmul_mx(
-                    out=outs[m],
-                    lhsT=w2c[:, P * m : P * m + P].bitcast(FP8X4),
-                    lhsT_scale=w2b[:, P * m : P * m + P],
-                    rhs=hc[:, 0:n].bitcast(FP8X4),
-                    rhs_scale=hb[:, 0:n],
+                    out=targets[m],
+                    lhsT=w2_words[:, P * m : P * m + P].bitcast(FP8X4),
+                    lhsT_scale=w2_bytes[:, P * m : P * m + P],
+                    rhs=words[:].bitcast(FP8X4),
+                    rhs_scale=scale_bytes[:],
                     start=True,
                     stop=True,
                 )
+            cols = slice(n0, n0 + BLOCK)
             if last:
-                yo0 = ring.tile([P, n], F32, name="yo0")
-                yo1 = ring.tile([P, n], F32, name="yo1")
-                nc.scalar.activation(yo0[:], outs[0], COPY)
-                nc.sync.dma_start(outv[:, 0, n0 : n0 + n], yo0[:])
-                nc.vector.tensor_copy(yo1[:], outs[1])
-                nc.sync.dma_start(outv[:, 1, n0 : n0 + n], yo1[:])
+                nc.scalar.activation(result[:, 0, :], targets[0], COPY)
+                nc.sync.dma_start(out_rows[:, 0, cols], result[:, 0, :])
+                nc.vector.tensor_copy(result[:, 1, :], targets[1])
+                nc.sync.dma_start(out_rows[:, 1, cols], result[:, 1, :])
             else:
-                yo = ring.tile([P, 2, n], F32, name="yo")
-                nc.scalar.activation(yo[:], y[:], COPY)
-                nc.sync.dma_start(outv[:, :, n0 : n0 + n], yo[:])
+                nc.scalar.activation(result[:], bank[:], COPY)
+                nc.sync.dma_start(out_rows[:, :, cols], result[:])
 
-        blocks = [2, 2, 2, 1, 1]
-        pend = None
-
-        def finish(item):
-            k, n, h = item
-            hc = ring.tile([P, 256], U32, name="hc", align_bytes=256)
-            hb = ring.tile([P, 256], U8, name="hb", align_bytes=256)
-            nc.vector.quantize_mx(
-                out=hc[:, 0 : P * n].bitcast(FP8X4),
-                scales=hb[:, 0 : P * n],
-                in_=h[:, 0 : P * n, :].rearrange("p n t -> p (n t)"),
-            )
-            layer2(P * k, P * n, hc, hb)
-
-        k = 0
-        for n in blocks:
-            h = ring.tile([P, 256, 4], BF16, name="h", align_bytes=256)
-            for r in range(n):
-                up_mul(k + r, h[:, P * r : P * r + P, :])
-                if pend:
-                    finish(pend)
-                    pend = None
-            pend = (k, n, h)
-            k += n
-        finish(pend)
+        waiting = None
+        for n0 in range(0, S, BLOCK):
+            hidden = ring.tile([P, BLOCK, PACK], BF16, name="hidden", align_bytes=256)
+            for a in range(0, BLOCK, P):
+                hidden_tokens(hidden[:, a : a + P, :], n0 + a)
+                if waiting:
+                    second_layer(*waiting)
+                    waiting = None
+            waiting = (n0, hidden)
+        second_layer(*waiting)

from contextlib import ExitStack

import concourse.mybir as mybir

K, T, S, H, N = 1024, 2048, 1024, 512, 256
FLOPS = 2 * S * (2 * K * H + H * N)

F32 = mybir.dt.float32
BF16 = mybir.dt.bfloat16
U32 = mybir.dt.uint32
U16 = mybir.dt.uint16
U8 = mybir.dt.uint8
FP8X4 = mybir.dt.float8_e4m3fn_x4
COPY = mybir.ActivationFunctionType.Copy
SILU = mybir.ActivationFunctionType.Silu
MULT = mybir.AluOpType.mult

P = 128
PACK = 4
KP = P * PACK
CHUNK = 512
HALF = 512
BLOCK = 256

TOKEN_LOADS = ((1024, 1024), (1024, 512, 512))
X_SCALAR = 288
W_SCALAR = {"w1_0": 384, "w1_1": 320, "w3_0": 384, "w3_1": 0}
W2_SCALAR = 128


def tile_picked_pick_glu_silu_sub_e_kernel(tc, xT, w1, w3, w2, offs, out):
    nc = tc.nc
    with ExitStack() as ctx:
        keep = ctx.enter_context(tc.tile_pool(name="keep", bufs=1))
        chunks = ctx.enter_context(tc.tile_pool(name="chunks", bufs=2))
        turns = ctx.enter_context(tc.tile_pool(name="turns", bufs=1))
        ring = ctx.enter_context(tc.tile_pool(name="ring", bufs=3))
        gate_banks = ctx.enter_context(tc.psum_pool(name="gate_banks", bufs=3))
        up_banks = ctx.enter_context(tc.psum_pool(name="up_banks", bufs=3))
        out_banks = ctx.enter_context(tc.psum_pool(name="out_banks", bufs=2))

        offsets = keep.tile([P, S // 16], U16, name="offsets")

        token_bytes = keep.tile([P, T], U8, name="token_bytes", align_bytes=256)
        nc.gpsimd.memset(token_bytes[:], 0)

        first = keep.tile([P, 16], F32, name="first")
        nc.gpsimd.memset(first[:], 0.0)
        nc.scalar.activation(first[:], first[:], SILU)

        def load(source, name):
            tile = keep.tile([P, PACK, source.shape[1]], F32, name=name)
            nc.sync.dma_start(tile[:], source.rearrange("(p j) c -> p j c", j=PACK))
            return tile

        token_rows = {}
        for s in range(2):
            start = 0
            for width in TOKEN_LOADS[s]:
                tile = load(xT[KP * s : KP * s + KP, start : start + width], "x_%d_%d" % (s, start))
                for a in range(0, width, CHUNK):
                    token_rows[s, (start + a) // CHUNK] = tile[:, :, a : a + CHUNK]
                if (s, start) == (0, 0):
                    nc.sync.dma_start(offsets[:], offs)
                start += width
        weight_rows = {}
        for name, w in (("w1", w1), ("w3", w3)):
            for s in range(2):
                key = "%s_%d" % (name, s)
                weight_rows[key] = load(w[KP * s : KP * s + KP, :], key)
        w2_rows = load(w2, "w2")

        def round_columns(grouped, rows, split):
            width = rows.shape[2]
            for a, b in ((0, split), (split, width)):
                if a < b:
                    dst = grouped[:, a:b, :].rearrange("p (c i) j -> p c j i", i=4)
                    src = rows[:, :, a:b].rearrange("p j (c i) -> p c j i", i=4)
                    if a == 0:
                        nc.scalar.activation(dst, src, COPY)
                    else:
                        nc.vector.tensor_copy(dst, src)

        def round_channels(grouped, rows, split):
            dst = grouped[:].rearrange("p t m j -> p m j t")
            src = rows[:].rearrange("p j (m t) -> p m j t", t=PACK)
            a = split // PACK
            if a > 0:
                nc.scalar.activation(dst[:, 0:a], src[:, 0:a], COPY)
            if a < P:
                nc.vector.tensor_copy(dst[:, a:P], src[:, a:P])

        def quantise(words, scale_bytes, grouped):
            nc.vector.quantize_mx(out=words.bitcast(FP8X4), scales=scale_bytes, in_=grouped)

        token_words = [keep.tile([P, T], U32, name="token_words_%d" % s, align_bytes=256) for s in range(2)]

        def quantise_tokens(s, c, grouped):
            cols = slice(CHUNK * c, CHUNK * c + CHUNK)
            quantise(
                token_words[s][:, cols], token_bytes[PACK * s : P, cols], grouped.rearrange("p c j -> p (c j)")
            )

        weight_codes = {}

        def quantise_weight(key, grouped):
            words = keep.tile([P, H], U32, name="words_" + key, align_bytes=256)
            scale_bytes = keep.tile([P, H], U8, name="bytes_" + key, align_bytes=256)
            quantise(words[:], scale_bytes[:], grouped[:].rearrange("p t m j -> p (t m j)"))
            weight_codes[key] = (words, scale_bytes)

        def gather(dst, window, first_entry):
            entries = offsets[:, first_entry // 16 : (first_entry + HALF) // 16]
            nc.vector.tensor_copy(dst, window[:].indirect(entries))

        last_chunks = turns.tile([P, 2 * CHUNK, PACK], BF16, name="last_chunks", align_bytes=256, offset=0)

        picked_words0 = keep.tile([P, S], U32, name="picked_words0", align_bytes=256)
        waiting = None
        for s in range(2):
            for c in range(T // CHUNK):
                if s == 1 and c >= 2:
                    grouped = last_chunks[:, CHUNK * (c - 2) : CHUNK * (c - 1), :]
                else:
                    chunk = chunks.tile([P, CHUNK, PACK], BF16, name="chunk", align_bytes=256)
                    grouped = chunk[:, :, :]
                round_columns(grouped, token_rows[s, c], X_SCALAR)
                if waiting:
                    quantise_tokens(*waiting)
                waiting = (s, c, grouped)
                if s == 1 and c in (1, 2):
                    gather(picked_words0[:, HALF * (c - 1) : HALF * c], token_words[0], HALF * (c - 1))
        quantise_tokens(*waiting)

        def grouped_weight(key, offset):
            grouped = turns.tile([P, PACK, P, PACK], BF16, name="grouped_" + key, align_bytes=256, offset=offset)
            round_channels(grouped, weight_rows[key], W_SCALAR[key])
            return grouped

        words1_a = keep.tile([P, HALF], U32, name="words1_a", align_bytes=256)
        bytes_a = keep.tile([P, HALF], U8, name="bytes_a", align_bytes=256)
        gather(words1_a[:], token_words[1], 0)
        gather(bytes_a[:], token_bytes, 0)
        grouped_w1_0 = grouped_weight("w1_0", 0)
        grouped_w1_1 = grouped_weight("w1_1", 4096)
        quantise_weight("w1_0", grouped_w1_0)
        quantise_weight("w1_1", grouped_w1_1)
        grouped_w3_0 = grouped_weight("w3_0", 0)
        words1_b = turns.tile([P, HALF], U32, name="words1_b", align_bytes=256, offset=4096)
        bytes_b = turns.tile([P, HALF], U8, name="bytes_b", align_bytes=256, offset=6144)
        gather(words1_b[:], token_words[1], HALF)
        gather(bytes_b[:], token_bytes, HALF)
        grouped_w3_1 = grouped_weight("w3_1", 6656)
        quantise_weight("w3_0", grouped_w3_0)
        quantise_weight("w3_1", grouped_w3_1)
        picked = ((words1_a, bytes_a), (words1_b, bytes_b))

        def first_layer(bank, name, t, n0, n):
            half, a = divmod(n0, HALF)
            words1, scale_bytes = picked[half]
            moving = (picked_words0[:, n0 : n0 + n], words1[:, a : a + n])
            cols = slice(P * t, P * t + P)
            for s in range(2):
                words, weight_bytes = weight_codes["%s_%d" % (name, s)]
                nc.tensor.matmul_mx(
                    out=bank,
                    lhsT=words[:, cols].bitcast(FP8X4),
                    lhsT_scale=weight_bytes[:, cols],
                    rhs=moving[s].bitcast(FP8X4),
                    rhs_scale=scale_bytes[PACK * s : P, a : a + n],
                    start=s == 0,
                    stop=s == 1,
                )

        gates = []
        for half in range(2):
            gate = keep.tile([P, PACK, HALF], F32, name="gate_%d" % half)
            for t in range(PACK):
                gate_bank = gate_banks.tile([P, HALF], F32, name="gate_bank")
                first_layer(gate_bank[:], "w1", t, HALF * half, HALF)
                nc.scalar.activation(gate[:, t, :], gate_bank[:], SILU)
            gates.append(gate)

        grouped_w2 = turns.tile([P, N, PACK], BF16, name="grouped_w2", align_bytes=256, offset=0)
        round_columns(grouped_w2[:, :, :], w2_rows[:, :, :], W2_SCALAR)
        w2_words = keep.tile([P, N], U32, name="w2_words", align_bytes=256)
        w2_bytes = keep.tile([P, N], U8, name="w2_bytes", align_bytes=256)
        quantise(w2_words[:], w2_bytes[:], grouped_w2[:].rearrange("p c j -> p (c j)"))

        out_rows = out.rearrange("(m p) n -> p m n", p=P)

        def hidden_tokens(hidden, n0):
            up_bank = up_banks.tile([P, PACK, P], F32, name="up_bank")
            for t in range(PACK):
                first_layer(up_bank[:, t, :], "w3", t, n0, P)
            half, a = divmod(n0, HALF)
            nc.vector.tensor_tensor(
                hidden.rearrange("p (c i) t -> p c t i", i=4),
                up_bank[:].rearrange("p t (c i) -> p c t i", i=4),
                gates[half][:, :, a : a + P].rearrange("p t (c i) -> p c t i", i=4),
                MULT,
            )

        def second_layer(n0, hidden):
            words = ring.tile([P, BLOCK], U32, name="hidden_words", align_bytes=256)
            scale_bytes = ring.tile([P, BLOCK], U8, name="hidden_bytes", align_bytes=256)
            quantise(words[:], scale_bytes[:], hidden[:].rearrange("p n t -> p (n t)"))
            result = ring.tile([P, N // P, BLOCK], F32, name="result")
            last = n0 + BLOCK == S
            if last:
                banks = [out_banks.tile([P, BLOCK], F32, name="out_half_%d" % m, tag="out_bank") for m in range(2)]
                targets = [bank[:] for bank in banks]
            else:
                bank = out_banks.tile([P, N // P, BLOCK], F32, name="out_bank", tag="out_bank")
                targets = [bank[:, m, :] for m in range(2)]
            for m in range(2):
                nc.tensor.matmul_mx(
                    out=targets[m],
                    lhsT=w2_words[:, P * m : P * m + P].bitcast(FP8X4),
                    lhsT_scale=w2_bytes[:, P * m : P * m + P],
                    rhs=words[:].bitcast(FP8X4),
                    rhs_scale=scale_bytes[:],
                    start=True,
                    stop=True,
                )
            cols = slice(n0, n0 + BLOCK)
            if last:
                nc.scalar.activation(result[:, 0, :], targets[0], COPY)
                nc.sync.dma_start(out_rows[:, 0, cols], result[:, 0, :])
                nc.vector.tensor_copy(result[:, 1, :], targets[1])
                nc.sync.dma_start(out_rows[:, 1, cols], result[:, 1, :])
            else:
                nc.scalar.activation(result[:], bank[:], COPY)
                nc.sync.dma_start(out_rows[:, :, cols], result[:])

        waiting = None
        for n0 in range(0, S, BLOCK):
            hidden = ring.tile([P, BLOCK, PACK], BF16, name="hidden", align_bytes=256)
            for a in range(0, BLOCK, P):
                hidden_tokens(hidden[:, a : a + P, :], n0 + a)
                if waiting:
                    second_layer(*waiting)
                    waiting = None
            waiting = (n0, hidden)
        second_layer(*waiting)
